import numpy as np
import ml_dtypes


def mxq(x, axis, fmt="e4m3"):
    dtype, down = {"e4m3": (ml_dtypes.float8_e4m3fn, 7), "e5m2": (ml_dtypes.float8_e5m2, 14)}[fmt]
    v = np.moveaxis(np.asarray(x, np.float32).astype(ml_dtypes.bfloat16).astype(np.float64), axis, -1)
    blocks = v.reshape(v.shape[:-1] + (-1, 32))
    amax = np.abs(blocks).max(-1, keepdims=True)
    byte = np.maximum(np.where(amax > 0, np.frexp(amax)[1] - 1 + 127, 0) - down, 1)
    scale = np.exp2(byte - 127.0)
    codes = (blocks / scale).astype(np.float32).astype(dtype).astype(np.float64)
    return np.moveaxis((codes * scale).reshape(v.shape), -1, axis)


WIDE = False


def mx_kscale(k):
    if not WIDE:
        return np.ones(k)
    levels = np.array([10, -10, 5, -5, 0])
    if k % 512:
        return np.exp2(np.random.permutation(np.resize(levels, k // 32))).repeat(32)
    a = np.empty((k // 512, 16))
    for p in range(k // 512):
        a[p, :8] = np.random.permutation(np.resize(levels, 8))
        for g in range(8):
            far = levels[np.abs(levels - a[p, g]) >= 10]
            a[p, g + 8] = far[np.random.randint(len(far))]
    return np.exp2(a.ravel()).repeat(32)


BF16 = ml_dtypes.bfloat16


def bf(x):
    return np.asarray(x, np.float32).astype(BF16)


def f64(x):
    return np.asarray(x).astype(np.float64)

E4M3FN = np.array([(-1.0 if i & 128 else 1.0) * ((1.0 + (i & 7) / 8.0) * 2.0 ** (((i >> 3) & 15) - 7) if i & 120 else (i & 7) * 2.0 ** -9) for i in range(256)])


def e4m3fn_bytes(y):
    return np.clip(np.asarray(y, np.float64), -448.0, 448.0).astype(np.float32).astype(ml_dtypes.float8_e4m3fn).view(np.uint8)


def e4m3fn_values(b):
    return E4M3FN[b]

def planes(Y):
    n, m = Y.shape
    b = f64(bf(Y)).reshape(n // 32, 32, m)
    amax = np.abs(b).max(1)
    byte = np.clip(np.where(amax > 0, np.frexp(amax)[1] - 1 + 127 - 7, 1), 1, 254)
    codes = (b * np.exp2(127.0 - byte)[:, None, :]).reshape(n, m).astype(np.float32).astype(ml_dtypes.float8_e4m3fn).view(np.uint8)
    words = codes.reshape(n // 512, 128, 4, m).transpose(0, 1, 3, 2)
    return np.ascontiguousarray(words), np.ascontiguousarray(byte.astype(np.uint8).reshape(n // 512, 16, m))


T, D, C, N, B = 2048, 256, 512, 1024, 128

def setup_inputs():
    s = mx_kscale(C)
    X = np.random.randn(T + D, C) * np.exp(0.3 * np.random.randn(T + D, 1)) * s
    X_scale = (np.abs(X).reshape(T + D, C // B, B).max(axis=2) / 448.0).astype(np.float32)
    X_bytes = e4m3fn_bytes(X / np.repeat(f64(X_scale), B, axis=1))
    return {
        "X_bytes": X_bytes,
        "X_scale": X_scale,
        "Wf_past": bf(np.random.randn(C, N) / np.sqrt(2 * C) / s[:, None]),
        "Wf_now": bf(np.random.randn(C, N) / np.sqrt(2 * C) / s[:, None]),
        "Wg_past": bf(np.random.randn(C, N) / np.sqrt(2 * C) / s[:, None]),
        "Wg_now": bf(np.random.randn(C, N) / np.sqrt(2 * C) / s[:, None]),
        "gain": bf(2.0 * np.exp(0.8 * np.random.randn(1, N))),
    }

def reference(X_bytes, X_scale, Wf_past, Wf_now, Wg_past, Wg_now, gain):
    X = e4m3fn_values(X_bytes) * np.repeat(f64(X_scale), B, axis=1)
    Xq = mxq(X, 1, "e4m3")
    filt = (Xq[:T] @ mxq(f64(Wf_past), 0, "e4m3")) + (Xq[D:] @ mxq(f64(Wf_now), 0, "e4m3"))
    gate = (Xq[:T] @ mxq(f64(Wg_past), 0, "e4m3")) + (Xq[D:] @ mxq(f64(Wg_now), 0, "e4m3"))
    y = np.tanh(filt) * (1.0 / (1.0 + np.exp(-gate))) * f64(gain)
    words, scales = planes(y.T)
    return y, words, scales

@@ -1,0 +1,372 @@
+from contextlib import ExitStack
+
+import concourse.mybir as mybir
+from concourse.masks import make_identity
+
+T, D, C, N = 2048, 256, 512, 1024
+FLOPS = 4 * 2 * T * C * N
+
+F32 = mybir.dt.float32
+BF16 = mybir.dt.bfloat16
+U32 = mybir.dt.uint32
+I32 = mybir.dt.int32
+U8 = mybir.dt.uint8
+FP8 = mybir.dt.float8_e4m3fn
+FP8X4 = mybir.dt.float8_e4m3fn_x4
+ACT = mybir.ActivationFunctionType
+ALU = mybir.AluOpType
+
+P = 128
+PACK = 4
+SEG = 256
+NSEG = (T + D) // SEG
+CHUNK = 512
+NCHUNK = T // CHUNK
+GROUP = P * PACK
+NGROUP = N // GROUP
+Y_EVAC_SCALAR = [2, 4, 3, 4, 3, 3, 2]
+ITEMS = [[("w", 0)], [("w", 1), ("w", 2)], [("w", 3), ("y", 0)], [("y", 1), ("y", 2)], [("y", 3), ("y", 4)], [("y", 5)]]
+TAIL = (256, 256)
+FOURCOL = False
+
+
+def tile_dilated_gated_activation_b1_kernel(
+    tc, X_bytes, X_scale, Wf_past, Wf_now, Wg_past, Wg_now, gain, out_0, out_1, out_2
+):
+    nc = tc.nc
+    weights = (Wf_past, Wf_now, Wg_past, Wg_now)
+
+    with ExitStack() as ctx:
+        keep = ctx.enter_context(tc.tile_pool(name="keep", bufs=1))
+        work = ctx.enter_context(tc.tile_pool(name="work", bufs=2))
+        psum = ctx.enter_context(tc.psum_pool(name="psum", bufs=4))
+        ctx.enter_context(tc.manual_schedule())
+
+        ident = keep.tile([P, P], F32, name="ident")
+        make_identity(nc, ident[:])
+        warm_in = keep.tile([P, 1], F32, name="warm_in")
+        warm_out = keep.tile([P, 1], F32, name="warm_out")
+        nc.vector.memset(warm_in[:], 0.0)
+        nc.scalar.activation(out=warm_out[:], in_=warm_in[:], func=ACT.Sigmoid)
+
+        x_rows = X_bytes.rearrange("(s p e) k -> p s (e k)", p=P, e=2)
+        x_bytes = {}
+
+        def load_x(first, last):
+            tile = keep.tile([P, last - first, 2 * C], U8, name="x_bytes_%d" % first)
+            nc.sync.dma_start(out=tile[:], in_=x_rows[:, first:last, :])
+            for s in range(first, last):
+                x_bytes[s] = tile[:, s - first, :]
+
+        w_raw = {}
+
+        def load_w(w, g):
+            tile = keep.tile([P, PACK, GROUP], BF16, name="w_raw_%d_%d" % (w, g))
+            nc.sync.dma_start(
+                out=tile[:],
+                in_=weights[w][:, g * GROUP : (g + 1) * GROUP].rearrange("(p j) n -> p j n", j=PACK),
+            )
+            w_raw[w, g] = tile
+
+        x_scale = keep.tile([P, NSEG, 8], F32, name="x_scale")
+        nc.sync.dma_start(out=x_scale[:], in_=X_scale.rearrange("(s p e) b -> p s (e b)", p=P, e=2))
+        load_x(0, 3)
+        for w in range(4):
+            load_w(w, 0)
+        gain_bf = keep.tile([P, NGROUP, PACK], BF16, name="gain_bf")
+        nc.sync.dma_start(out=gain_bf[:], in_=gain.rearrange("o (g p t) -> p (o g) t", p=P, t=PACK))
+        load_x(3, 5)
+        load_x(5, 9)
+        for w in range(4):
+            load_w(w, 1)
+
+        x_codes = keep.tile([P, T + D], U32, name="x_codes", align_bytes=64)
+        x_planes = keep.tile([P, T + D], U8, name="x_planes", align_bytes=64)
+        x_wide, x_bank, x_grouped = {}, {}, {}
+
+        def widen(s, on_scalar):
+            tile = work.tile([P, 2, C], BF16, name="x_wide", bufs=4)
+            x_wide[s] = (tile, on_scalar)
+            for e in range(2):
+                for b in range(4):
+                    src = x_bytes[s][:, e * C + 128 * b : e * C + 128 * (b + 1)].bitcast(FP8)
+                    scale = x_scale[:, s, 4 * e + b : 4 * e + b + 1]
+                    if on_scalar:
+                        nc.scalar.activation(
+                            out=tile[:, e, 128 * b : 128 * (b + 1)], in_=src, func=ACT.Copy, scale=scale
+                        )
+                    else:
+                        dst = tile[:, e, :].rearrange("q (u p h) -> q p u h", u=2, h=2)
+                        nc.vector.tensor_scalar(
+                            out=dst[:, 32 * b : 32 * (b + 1), :, :],
+                            in0=src.rearrange("q (p u h) -> q p u h", u=2, h=2),
+                            scalar1=scale,
+                            scalar2=None,
+                            op0=ALU.mult,
+                        )
+
+        def turn_x(s):
+            tile, natural = x_wide[s]
+            bank = psum.tile([P, 2, 2, P], F32, name="turn_bank")
+            x_bank[s] = bank
+            for e in range(2):
+                words = tile[:, e, :].bitcast(F32)
+                for u in range(2):
+                    src = words[:, u : 2 * P : 2] if natural else words[:, u * P : (u + 1) * P]
+                    nc.tensor.transpose(bank[:, e, u, :], src, ident[:])
+
+        def empty_x(s):
+            tile = work.tile([P, SEG * PACK], BF16, name="x_grouped", bufs=4, align_bytes=64)
+            x_grouped[s] = tile
+            nc.scalar.copy(
+                out=tile[:].bitcast(F32).rearrange("p (r e u) -> p r e u", e=2, u=2),
+                in_=x_bank[s][:].rearrange("p e u r -> p r e u"),
+            )
+
+        def quantise_x(s):
+            cols = slice(s * SEG, (s + 1) * SEG)
+            nc.vector.quantize_mx(
+                out=x_codes[:, cols].bitcast(FP8X4), scales=x_planes[:, cols], in_=x_grouped[s][:]
+            )
+
+        w_grouped, w_codes, w_planes = {}, {}, {}
+
+        def group_w(w, g, on_scalar=False):
+            tile = work.tile([P, GROUP * PACK], BF16, name="w_grouped", bufs=3, align_bytes=64)
+            w_grouped[w, g] = tile
+            dst = tile[:].rearrange("p (t a b j) -> p a t b j", t=PACK, b=2, j=PACK)
+            src = w_raw[w, g][:].rearrange("p j (a b t) -> p a t b j", b=2, t=PACK)
+            if on_scalar:
+                nc.scalar.copy(out=dst, in_=src)
+            else:
+                nc.vector.tensor_copy(out=dst, in_=src)
+
+        def quantise_w(w, g):
+            codes = keep.tile([P, GROUP], U32, name="w_codes_%d_%d" % (w, g), align_bytes=64)
+            planes = keep.tile([P, GROUP], U8, name="w_planes_%d_%d" % (w, g), align_bytes=64)
+            w_codes[w, g], w_planes[w, g] = codes, planes
+            nc.vector.quantize_mx(out=codes[:].bitcast(FP8X4), scales=planes[:], in_=w_grouped[w, g][:])
+
+        units = [(g, c * CHUNK, CHUNK) for g in range(NGROUP) for c in range(NCHUNK)]
+        tail_g, tail_tok = units.pop()[:2]
+        for n in TAIL:
+            units.append((tail_g, tail_tok, n))
+            tail_tok = tail_tok + n
+        acts, y_tiles, y_banks = {}, {}, {}
+
+        def steps(i):
+            return PACK * units[i][2] // CHUNK
+
+        def conv(i, k, half):
+            g, tok, n = units[i]
+            per = CHUNK // n
+            bank = psum.tile([P, per, n], F32, name="conv_bank")
+            for r in range(per):
+                t = k * per + r
+                cols = slice(t * P, (t + 1) * P)
+                for tap in range(2):
+                    w = 2 * half + tap
+                    toks = slice(tok + tap * D, tok + n + tap * D)
+                    nc.tensor.matmul_mx(
+                        out=bank[:, r, :],
+                        lhsT=w_codes[w, g][:, cols].bitcast(FP8X4),
+                        lhsT_scale=w_planes[w, g][:, cols],
+                        rhs=x_codes[:, toks].bitcast(FP8X4),
+                        rhs_scale=x_planes[:, toks],
+                        start=(tap == 0),
+                        stop=(tap == 1),
+                    )
+            tile = work.tile([P, per, n], F32, name=("tanh_f", "sig_h")[half], bufs=4)
+            acts[i, k, half] = tile
+            nc.scalar.activation(out=tile[:], in_=bank[:], func=(ACT.Tanh, ACT.Sigmoid)[half])
+
+        def gate(i, k):
+            conv(i, k, 0)
+            conv(i, k, 1)
+
+        def product(i, k):
+            g, tok, n = units[i]
+            per = CHUNK // n
+            if k == 0:
+                y_tiles[i] = work.tile([P, PACK, n], F32, name="y_tile", bufs=6)
+            for r in range(per):
+                t = k * per + r
+                nc.vector.scalar_tensor_tensor(
+                    out=y_tiles[i][:, t, :],
+                    in0=acts[i, k, 0][:, r, :],
+                    scalar=gain_bf[:, g, t : t + 1],
+                    in1=acts[i, k, 1][:, r, :],
+                    op0=ALU.mult,
+                    op1=ALU.mult,
+                )
+
+        def turn_y(i, slots=range(PACK)):
+            for j in range(steps(i)):
+                if (i, j) not in y_banks:
+                    y_banks[i, j] = psum.tile([P, PACK, P], F32, name="turn_bank")
+                for t in slots:
+                    nc.tensor.transpose(y_banks[i, j][:, t, :], y_tiles[i][:, t, j * P : (j + 1) * P], ident[:])
+
+        def empty_y(i, j, on_scalar):
+            g, tok, n = units[i]
+            tile = work.tile([P, GROUP], F32, name="y_rows", bufs=6)
+            dst = tile[:].rearrange("q (p t) -> q p t", t=PACK)
+            src = y_banks[i, j][:].rearrange("q t p -> q p t")
+            if on_scalar:
+                nc.scalar.copy(out=dst, in_=src)
+            else:
+                nc.vector.tensor_copy(out=dst, in_=src)
+            row = tok + j * P
+            nc.sync.dma_start(out=out_0[row : row + P, g * GROUP : (g + 1) * GROUP], in_=tile[:])
+
+        y_grouped = {}
+        y_planes = []
+        for g in range(NGROUP):
+            plane = keep.tile([P, T], U8, name="y_planes_%d" % g, align_bytes=64)
+            y_planes.append(plane)
+
+        def round_y(i):
+            n = units[i][2]
+            tile = work.tile([P, n * PACK], BF16, name="y_grouped", bufs=2, align_bytes=64)
+            y_grouped[i] = tile
+            if FOURCOL:
+                nc.vector.tensor_copy(
+                    out=tile[:].rearrange("p (c i t) -> p c t i", t=PACK, i=4),
+                    in_=y_tiles[i][:].rearrange("p t (c i) -> p c t i", i=4),
+                )
+            else:
+                nc.vector.tensor_copy(
+                    out=tile[:].rearrange("p (m t) -> p m t", t=PACK), in_=y_tiles[i][:].rearrange("p t m -> p m t")
+                )
+
+        def quantise_y(i):
+            g, tok, n = units[i]
+            toks = slice(tok, tok + n)
+            codes = work.tile([P, n], U32, name="y_codes", bufs=3, align_bytes=64)
+            nc.vector.quantize_mx(out=codes[:].bitcast(FP8X4), scales=y_planes[g][:, toks], in_=y_grouped[i][:])
+            words = out_1[g].rearrange("p m t -> p (m t)").bitcast(I32)
+            nc.sync.dma_start(out=words[:, toks], in_=codes[:].bitcast(I32))
+            if tok + n == T:
+                for q in range(4):
+                    queue = nc.scalar if (g == NGROUP - 1 and q % 2 == 1) else nc.sync
+                    queue.dma_start(
+                        out=out_2[g, 4 * q : 4 * q + 4, :].bitcast(I32),
+                        in_=y_planes[g][32 * q : 32 * q + 4, :].bitcast(I32),
+                    )
+
+        widen(0, False)
+        widen(1, True)
+        widen(2, True)
+        turn_x(0)
+        empty_x(0)
+        group_w(0, 0)
+        turn_x(1)
+        empty_x(1)
+        turn_x(2)
+        empty_x(2)
+        quantise_x(0)
+        quantise_w(0, 0)
+        group_w(1, 0)
+        group_w(2, 0, True)
+        quantise_x(1)
+        quantise_w(1, 0)
+        quantise_x(2)
+        for t in range(PACK):
+            conv(0, t, 0)
+        group_w(3, 0)
+        quantise_w(2, 0)
+        widen(3, False)
+        quantise_w(3, 0)
+        widen(4, False)
+        turn_x(3)
+        empty_x(3)
+        conv(0, 0, 1)
+        conv(0, 1, 1)
+        turn_x(4)
+        empty_x(4)
+        widen(5, False)
+        product(0, 0)
+        quantise_x(3)
+        widen(6, False)
+        quantise_x(4)
+        conv(0, 2, 1)
+        conv(0, 3, 1)
+        product(0, 1)
+        turn_x(5)
+        turn_x(6)
+        empty_x(5)
+        empty_x(6)
+        product(0, 2)
+
+        def item(kind, k):
+            if kind == "w":
+                return (lambda: group_w(k, 1), lambda: quantise_w(k, 1))
+            return (lambda: round_y(k), lambda: quantise_y(k))
+
+        full = NGROUP * NCHUNK - 1
+        for i in range(1, full):
+            items = [item(kind, k) for kind, k in ITEMS[i - 1]]
+            side = [[], [], [], []]
+            if i in (1, 2):
+                side[0].extend([lambda: quantise_x(2 * i + 3), lambda: quantise_x(2 * i + 4)])
+            side[0].append(items[0][0])
+            side[1].append(items[0][1])
+            if len(items) > 1:
+                side[2].append(items[1][0])
+                side[3].append(items[1][1])
+            if i == 1:
+                side[2].extend([lambda: widen(7, False), lambda: widen(8, False)])
+            n_s = Y_EVAC_SCALAR[i - 1]
+            gate(i, 0)
+            gate(i, 1)
+            product(i - 1, 3)
+            turn_y(i - 1)
+            for f in side[0]:
+                f()
+            product(i, 0)
+            for f in side[1]:
+                f()
+            product(i, 1)
+            for j in range(n_s):
+                empty_y(i - 1, j, True)
+            for j in range(n_s, 4):
+                empty_y(i - 1, j, False)
+            gate(i, 2)
+            gate(i, 3)
+            for f in side[2]:
+                f()
+            if i == 1:
+                turn_x(7)
+                turn_x(8)
+                empty_x(7)
+                empty_x(8)
+            product(i, 2)
+            for f in side[3]:
+                f()
+
+        a, b = full, full + 1
+        gate(a, 0)
+        gate(a, 1)
+        product(a - 1, 3)
+        turn_y(a - 1)
+        round_y(a - 1)
+        product(a, 0)
+        quantise_y(a - 1)
+        product(a, 1)
+        n_s = Y_EVAC_SCALAR[a - 1]
+        for j in range(4):
+            empty_y(a - 1, j, j < n_s)
+        gate(b, 0)
+        gate(b, 1)
+        turn_y(a)
+        round_y(a)
+        product(b, 0)
+        quantise_y(a)
+        product(b, 1)
+        turn_y(b)
+        empty_y(a, 0, True)
+        empty_y(a, 1, True)
+        round_y(b)
+        empty_y(b, 0, True)
+        quantise_y(b)
+        empty_y(b, 1, True)

@@ -24,10 +24,11 @@ CHUNK = 512
 NCHUNK = T // CHUNK
 GROUP = P * PACK
 NGROUP = N // GROUP
-Y_EVAC_SCALAR = [2, 4, 3, 4, 3, 3, 2]
+Y_EVAC_SCALAR = [2, 4, 3, 4, 3, 2, 3]
 ITEMS = [[("w", 0)], [("w", 1), ("w", 2)], [("w", 3), ("y", 0)], [("y", 1), ("y", 2)], [("y", 3), ("y", 4)], [("y", 5)]]
 TAIL = (256, 256)
-FOURCOL = False
+FOURCOL = True
+LATE = True
 
 
 def tile_dilated_gated_activation_b1_kernel(
@@ -134,8 +135,12 @@ def tile_dilated_gated_activation_b1_kernel(
         def group_w(w, g, on_scalar=False):
             tile = work.tile([P, GROUP * PACK], BF16, name="w_grouped", bufs=3, align_bytes=64)
             w_grouped[w, g] = tile
-            dst = tile[:].rearrange("p (t a b j) -> p a t b j", t=PACK, b=2, j=PACK)
-            src = w_raw[w, g][:].rearrange("p j (a b t) -> p a t b j", b=2, t=PACK)
+            if FOURCOL:
+                dst = tile[:].rearrange("p (t a b j) -> p a j b t", t=PACK, b=2, j=PACK)
+                src = w_raw[w, g][:].rearrange("p j (a b t) -> p a j b t", b=2, t=PACK)
+            else:
+                dst = tile[:].rearrange("p (t a b j) -> p a t b j", t=PACK, b=2, j=PACK)
+                src = w_raw[w, g][:].rearrange("p j (a b t) -> p a t b j", b=2, t=PACK)
             if on_scalar:
                 nc.scalar.copy(out=dst, in_=src)
             else:
@@ -209,7 +214,7 @@ def tile_dilated_gated_activation_b1_kernel(
 
         def empty_y(i, j, on_scalar):
             g, tok, n = units[i]
-            tile = work.tile([P, GROUP], F32, name="y_rows", bufs=6)
+            tile = work.tile([P, GROUP], F32, name="y_rows", bufs=8)
             dst = tile[:].rearrange("q (p t) -> q p t", t=PACK)
             src = y_banks[i, j][:].rearrange("q t p -> q p t")
             if on_scalar:
@@ -260,34 +265,34 @@ def tile_dilated_gated_activation_b1_kernel(
         turn_x(0)
         empty_x(0)
         group_w(0, 0)
+        group_w(1, 0)
         turn_x(1)
         empty_x(1)
         turn_x(2)
         empty_x(2)
-        quantise_x(0)
         quantise_w(0, 0)
-        group_w(1, 0)
+        quantise_x(0)
+        quantise_w(1, 0)
         group_w(2, 0, True)
         quantise_x(1)
-        quantise_w(1, 0)
         quantise_x(2)
         for t in range(PACK):
             conv(0, t, 0)
         group_w(3, 0)
         quantise_w(2, 0)
-        widen(3, False)
         quantise_w(3, 0)
+        widen(3, False)
         widen(4, False)
-        turn_x(3)
-        empty_x(3)
         conv(0, 0, 1)
         conv(0, 1, 1)
+        turn_x(3)
         turn_x(4)
+        empty_x(3)
         empty_x(4)
         widen(5, False)
         product(0, 0)
-        quantise_x(3)
         widen(6, False)
+        quantise_x(3)
         quantise_x(4)
         conv(0, 2, 1)
         conv(0, 3, 1)
@@ -320,6 +325,8 @@ def tile_dilated_gated_activation_b1_kernel(
             gate(i, 0)
             gate(i, 1)
             product(i - 1, 3)
+            if LATE:
+                gate(i, 2)
             turn_y(i - 1)
             for f in side[0]:
                 f()
@@ -327,14 +334,19 @@ def tile_dilated_gated_activation_b1_kernel(
             for f in side[1]:
                 f()
             product(i, 1)
+            if LATE:
+                for f in side[2]:
+                    f()
             for j in range(n_s):
                 empty_y(i - 1, j, True)
             for j in range(n_s, 4):
                 empty_y(i - 1, j, False)
-            gate(i, 2)
+            if not LATE:
+                gate(i, 2)
             gate(i, 3)
-            for f in side[2]:
-                f()
+            if not LATE:
+                for f in side[2]:
+                    f()
             if i == 1:
                 turn_x(7)
                 turn_x(8)
@@ -362,11 +374,12 @@ def tile_dilated_gated_activation_b1_kernel(
         round_y(a)
         product(b, 0)
         quantise_y(a)
+        turn_y(b, (0, 1))
         product(b, 1)
-        turn_y(b)
+        turn_y(b, (2, 3))
         empty_y(a, 0, True)
         empty_y(a, 1, True)
         round_y(b)
         empty_y(b, 0, True)
-        quantise_y(b)
         empty_y(b, 1, True)
+        quantise_y(b)

@@ -18,17 +18,15 @@ ALU = mybir.AluOpType
 
 P = 128
 PACK = 4
-SEG = 256
-NSEG = (T + D) // SEG
-CHUNK = 512
-NCHUNK = T // CHUNK
 GROUP = P * PACK
 NGROUP = N // GROUP
-Y_EVAC_SCALAR = [2, 4, 3, 4, 3, 2, 3]
-ITEMS = [[("w", 0)], [("w", 1), ("w", 2)], [("w", 3), ("y", 0)], [("y", 1), ("y", 2)], [("y", 3), ("y", 4)], [("y", 5)]]
-TAIL = (256, 256)
-FOURCOL = True
-LATE = True
+BANK = 512
+NCHUNK = T // BANK
+SEG = 256
+NSEG = (T + D) // SEG
+SCALE_SPAN = 128
+NSCALE = C // SCALE_SPAN
+FILTER, GATE = 0, 1
 
 
 def tile_dilated_gated_activation_b1_kernel(
@@ -50,170 +48,171 @@ def tile_dilated_gated_activation_b1_kernel(
         nc.vector.memset(warm_in[:], 0.0)
         nc.scalar.activation(out=warm_out[:], in_=warm_in[:], func=ACT.Sigmoid)
 
-        x_rows = X_bytes.rearrange("(s p e) k -> p s (e k)", p=P, e=2)
-        x_bytes = {}
+        byte_rows = X_bytes.rearrange("(s p e) k -> p s (e k)", p=P, e=2)
+        scale_rows = X_scale.rearrange("(s p e) b -> p s (e b)", p=P, e=2)
+        x_bytes, x_scale, w_raw = {}, {}, {}
 
-        def load_x(first, last):
+        def load_bytes(first, last):
             tile = keep.tile([P, last - first, 2 * C], U8, name="x_bytes_%d" % first)
-            nc.sync.dma_start(out=tile[:], in_=x_rows[:, first:last, :])
+            nc.sync.dma_start(out=tile[:], in_=byte_rows[:, first:last, :])
             for s in range(first, last):
                 x_bytes[s] = tile[:, s - first, :]
 
-        w_raw = {}
+        def load_scale(first, last):
+            tile = keep.tile([P, last - first, 2 * NSCALE], F32, name="x_scale_%d" % first)
+            nc.sync.dma_start(out=tile[:], in_=scale_rows[:, first:last, :])
+            for s in range(first, last):
+                x_scale[s] = tile[:, s - first, :]
 
-        def load_w(w, g):
+        def load_weight(w, g):
             tile = keep.tile([P, PACK, GROUP], BF16, name="w_raw_%d_%d" % (w, g))
-            nc.sync.dma_start(
-                out=tile[:],
-                in_=weights[w][:, g * GROUP : (g + 1) * GROUP].rearrange("(p j) n -> p j n", j=PACK),
-            )
+            columns = weights[w][:, g * GROUP : (g + 1) * GROUP]
+            nc.sync.dma_start(out=tile[:], in_=columns.rearrange("(p j) n -> p j n", j=PACK))
             w_raw[w, g] = tile
 
-        x_scale = keep.tile([P, NSEG, 8], F32, name="x_scale")
-        nc.sync.dma_start(out=x_scale[:], in_=X_scale.rearrange("(s p e) b -> p s (e b)", p=P, e=2))
-        load_x(0, 3)
-        for w in range(4):
-            load_w(w, 0)
-        gain_bf = keep.tile([P, NGROUP, PACK], BF16, name="gain_bf")
-        nc.sync.dma_start(out=gain_bf[:], in_=gain.rearrange("o (g p t) -> p (o g) t", p=P, t=PACK))
-        load_x(3, 5)
-        load_x(5, 9)
-        for w in range(4):
-            load_w(w, 1)
+        load_scale(0, 5)
+        load_bytes(0, 3)
+        load_weight(0, 0)
+        load_weight(1, 0)
+        load_bytes(3, 5)
+        load_weight(2, 0)
+        load_weight(3, 0)
+        load_scale(5, NSEG)
+        gains = keep.tile([P, NGROUP, PACK], BF16, name="gains")
+        nc.sync.dma_start(out=gains[:], in_=gain.rearrange("o (g p t) -> p (o g) t", p=P, t=PACK))
+        load_bytes(5, NSEG)
+        for w in range(len(weights)):
+            load_weight(w, 1)
 
         x_codes = keep.tile([P, T + D], U32, name="x_codes", align_bytes=64)
-        x_planes = keep.tile([P, T + D], U8, name="x_planes", align_bytes=64)
-        x_wide, x_bank, x_grouped = {}, {}, {}
+        x_mxscale = keep.tile([P, T + D], U8, name="x_mxscale", align_bytes=64)
+        x_words, x_bank, x_grouped = {}, {}, {}
 
-        def widen(s, on_scalar):
+        def widen(s, on_scalar=False):
             tile = work.tile([P, 2, C], BF16, name="x_wide", bufs=4)
-            x_wide[s] = (tile, on_scalar)
+            x_words[s] = []
             for e in range(2):
-                for b in range(4):
-                    src = x_bytes[s][:, e * C + 128 * b : e * C + 128 * (b + 1)].bitcast(FP8)
-                    scale = x_scale[:, s, 4 * e + b : 4 * e + b + 1]
+                for b in range(NSCALE):
+                    span = slice(SCALE_SPAN * b, SCALE_SPAN * (b + 1))
+                    src = x_bytes[s][:, e * C : (e + 1) * C][:, span].bitcast(FP8)
+                    scale = x_scale[s][:, NSCALE * e + b : NSCALE * e + b + 1]
                     if on_scalar:
-                        nc.scalar.activation(
-                            out=tile[:, e, 128 * b : 128 * (b + 1)], in_=src, func=ACT.Copy, scale=scale
-                        )
+                        nc.scalar.activation(out=tile[:, e, span], in_=src, func=ACT.Copy, scale=scale)
                     else:
                         dst = tile[:, e, :].rearrange("q (u p h) -> q p u h", u=2, h=2)
                         nc.vector.tensor_scalar(
-                            out=dst[:, 32 * b : 32 * (b + 1), :, :],
+                            out=dst[:, SCALE_SPAN // PACK * b : SCALE_SPAN // PACK * (b + 1), :, :],
                             in0=src.rearrange("q (p u h) -> q p u h", u=2, h=2),
                             scalar1=scale,
                             scalar2=None,
                             op0=ALU.mult,
                         )
+                words = tile[:, e, :].bitcast(F32)
+                if on_scalar:
+                    x_words[s].append([words[:, u : 2 * P : 2] for u in range(2)])
+                else:
+                    x_words[s].append([words[:, u * P : (u + 1) * P] for u in range(2)])
 
         def turn_x(s):
-            tile, natural = x_wide[s]
-            bank = psum.tile([P, 2, 2, P], F32, name="turn_bank")
-            x_bank[s] = bank
+            x_bank[s] = psum.tile([P, 2, 2, P], F32, name="turn_bank")
             for e in range(2):
-                words = tile[:, e, :].bitcast(F32)
                 for u in range(2):
-                    src = words[:, u : 2 * P : 2] if natural else words[:, u * P : (u + 1) * P]
-                    nc.tensor.transpose(bank[:, e, u, :], src, ident[:])
+                    nc.tensor.transpose(x_bank[s][:, e, u, :], x_words[s][e][u], ident[:])
 
         def empty_x(s):
-            tile = work.tile([P, SEG * PACK], BF16, name="x_grouped", bufs=4, align_bytes=64)
-            x_grouped[s] = tile
+            x_grouped[s] = work.tile([P, SEG * PACK], BF16, name="x_grouped", bufs=4, align_bytes=64)
             nc.scalar.copy(
-                out=tile[:].bitcast(F32).rearrange("p (r e u) -> p r e u", e=2, u=2),
+                out=x_grouped[s][:].bitcast(F32).rearrange("p (r e u) -> p r e u", e=2, u=2),
                 in_=x_bank[s][:].rearrange("p e u r -> p r e u"),
             )
 
         def quantise_x(s):
             cols = slice(s * SEG, (s + 1) * SEG)
-            nc.vector.quantize_mx(
-                out=x_codes[:, cols].bitcast(FP8X4), scales=x_planes[:, cols], in_=x_grouped[s][:]
-            )
+            nc.vector.quantize_mx(out=x_codes[:, cols].bitcast(FP8X4), scales=x_mxscale[:, cols], in_=x_grouped[s][:])
 
-        w_grouped, w_codes, w_planes = {}, {}, {}
+        w_grouped, w_codes, w_mxscale = {}, {}, {}
 
         def group_w(w, g, on_scalar=False):
-            tile = work.tile([P, GROUP * PACK], BF16, name="w_grouped", bufs=3, align_bytes=64)
-            w_grouped[w, g] = tile
-            if FOURCOL:
-                dst = tile[:].rearrange("p (t a b j) -> p a j b t", t=PACK, b=2, j=PACK)
-                src = w_raw[w, g][:].rearrange("p j (a b t) -> p a j b t", b=2, t=PACK)
-            else:
-                dst = tile[:].rearrange("p (t a b j) -> p a t b j", t=PACK, b=2, j=PACK)
-                src = w_raw[w, g][:].rearrange("p j (a b t) -> p a t b j", b=2, t=PACK)
+            w_grouped[w, g] = work.tile([P, GROUP * PACK], BF16, name="w_grouped", bufs=3, align_bytes=64)
+            dst = w_grouped[w, g][:].rearrange("p (t a b j) -> p a j b t", t=PACK, b=2, j=PACK)
+            src = w_raw[w, g][:].rearrange("p j (a b t) -> p a j b t", b=2, t=PACK)
             if on_scalar:
                 nc.scalar.copy(out=dst, in_=src)
             else:
                 nc.vector.tensor_copy(out=dst, in_=src)
 
         def quantise_w(w, g):
-            codes = keep.tile([P, GROUP], U32, name="w_codes_%d_%d" % (w, g), align_bytes=64)
-            planes = keep.tile([P, GROUP], U8, name="w_planes_%d_%d" % (w, g), align_bytes=64)
-            w_codes[w, g], w_planes[w, g] = codes, planes
-            nc.vector.quantize_mx(out=codes[:].bitcast(FP8X4), scales=planes[:], in_=w_grouped[w, g][:])
+            w_codes[w, g] = keep.tile([P, GROUP], U32, name="w_codes_%d_%d" % (w, g), align_bytes=64)
+            w_mxscale[w, g] = keep.tile([P, GROUP], U8, name="w_mxscale_%d_%d" % (w, g), align_bytes=64)
+            nc.vector.quantize_mx(
+                out=w_codes[w, g][:].bitcast(FP8X4), scales=w_mxscale[w, g][:], in_=w_grouped[w, g][:]
+            )
 
-        units = [(g, c * CHUNK, CHUNK) for g in range(NGROUP) for c in range(NCHUNK)]
-        tail_g, tail_tok = units.pop()[:2]
-        for n in TAIL:
-            units.append((tail_g, tail_tok, n))
-            tail_tok = tail_tok + n
-        acts, y_tiles, y_banks = {}, {}, {}
+        units = [(g, c * BANK, BANK) for g in range(NGROUP) for c in range(NCHUNK)][:-1]
+        last_full = len(units) - 1
+        units.extend([(NGROUP - 1, T - BANK, BANK // 2), (NGROUP - 1, T - BANK // 2, BANK // 2)])
+        conv_banks, acts, y_tiles, y_banks, y_grouped = {}, {}, {}, {}, {}
 
-        def steps(i):
-            return PACK * units[i][2] // CHUNK
+        def tap_pass(i, k, conv, r, tap):
+            g, first, n = units[i]
+            if (i, k, conv) not in conv_banks:
+                conv_banks[i, k, conv] = psum.tile([P, BANK // n, n], F32, name="conv_bank")
+            t = k * (BANK // n) + r
+            cols = slice(t * P, (t + 1) * P)
+            steps = slice(first + tap * D, first + n + tap * D)
+            nc.tensor.matmul_mx(
+                out=conv_banks[i, k, conv][:, r, :],
+                lhsT=w_codes[2 * conv + tap, g][:, cols].bitcast(FP8X4),
+                lhsT_scale=w_mxscale[2 * conv + tap, g][:, cols],
+                rhs=x_codes[:, steps].bitcast(FP8X4),
+                rhs_scale=x_mxscale[:, steps],
+                start=(tap == 0),
+                stop=(tap == 1),
+            )
 
-        def conv(i, k, half):
-            g, tok, n = units[i]
-            per = CHUNK // n
-            bank = psum.tile([P, per, n], F32, name="conv_bank")
-            for r in range(per):
-                t = k * per + r
-                cols = slice(t * P, (t + 1) * P)
-                for tap in range(2):
-                    w = 2 * half + tap
-                    toks = slice(tok + tap * D, tok + n + tap * D)
-                    nc.tensor.matmul_mx(
-                        out=bank[:, r, :],
-                        lhsT=w_codes[w, g][:, cols].bitcast(FP8X4),
-                        lhsT_scale=w_planes[w, g][:, cols],
-                        rhs=x_codes[:, toks].bitcast(FP8X4),
-                        rhs_scale=x_planes[:, toks],
-                        start=(tap == 0),
-                        stop=(tap == 1),
-                    )
-            tile = work.tile([P, per, n], F32, name=("tanh_f", "sig_h")[half], bufs=4)
-            acts[i, k, half] = tile
-            nc.scalar.activation(out=tile[:], in_=bank[:], func=(ACT.Tanh, ACT.Sigmoid)[half])
+        def activate(i, k, conv):
+            n = units[i][2]
+            acts[i, k, conv] = work.tile([P, BANK // n, n], F32, name=("tanh_f", "sigmoid_h")[conv], bufs=4)
+            nc.scalar.activation(
+                out=acts[i, k, conv][:], in_=conv_banks[i, k, conv][:], func=(ACT.Tanh, ACT.Sigmoid)[conv]
+            )
 
-        def gate(i, k):
-            conv(i, k, 0)
-            conv(i, k, 1)
+        def convolve(i, k, convs=(FILTER, GATE)):
+            for conv in convs:
+                for r in range(BANK // units[i][2]):
+                    for tap in range(2):
+                        tap_pass(i, k, conv, r, tap)
+                activate(i, k, conv)
 
         def product(i, k):
-            g, tok, n = units[i]
-            per = CHUNK // n
+            g, first, n = units[i]
             if k == 0:
                 y_tiles[i] = work.tile([P, PACK, n], F32, name="y_tile", bufs=6)
-            for r in range(per):
-                t = k * per + r
+            for r in range(BANK // n):
+                t = k * (BANK // n) + r
                 nc.vector.scalar_tensor_tensor(
                     out=y_tiles[i][:, t, :],
-                    in0=acts[i, k, 0][:, r, :],
-                    scalar=gain_bf[:, g, t : t + 1],
-                    in1=acts[i, k, 1][:, r, :],
+                    in0=acts[i, k, FILTER][:, r, :],
+                    scalar=gains[:, g, t : t + 1],
+                    in1=acts[i, k, GATE][:, r, :],
                     op0=ALU.mult,
                     op1=ALU.mult,
                 )
 
         def turn_y(i, slots=range(PACK)):
-            for j in range(steps(i)):
+            for j in range(units[i][2] // P):
                 if (i, j) not in y_banks:
                     y_banks[i, j] = psum.tile([P, PACK, P], F32, name="turn_bank")
                 for t in slots:
                     nc.tensor.transpose(y_banks[i, j][:, t, :], y_tiles[i][:, t, j * P : (j + 1) * P], ident[:])
 
-        def empty_y(i, j, on_scalar):
-            g, tok, n = units[i]
+        def store_rows(i, on_scalar):
+            g, first, n = units[i]
+            for j in range(n // P):
+                store_row_bank(i, j, j < on_scalar)
+
+        def store_row_bank(i, j, on_scalar):
+            g, first, n = units[i]
             tile = work.tile([P, GROUP], F32, name="y_rows", bufs=8)
             dst = tile[:].rearrange("q (p t) -> q p t", t=PACK)
             src = y_banks[i, j][:].rearrange("q t p -> q p t")
@@ -221,155 +220,143 @@ def tile_dilated_gated_activation_b1_kernel(
                 nc.scalar.copy(out=dst, in_=src)
             else:
                 nc.vector.tensor_copy(out=dst, in_=src)
-            row = tok + j * P
+            row = first + j * P
             nc.sync.dma_start(out=out_0[row : row + P, g * GROUP : (g + 1) * GROUP], in_=tile[:])
 
-        y_grouped = {}
-        y_planes = []
+        y_mxscale = []
         for g in range(NGROUP):
-            plane = keep.tile([P, T], U8, name="y_planes_%d" % g, align_bytes=64)
-            y_planes.append(plane)
+            y_mxscale.append(keep.tile([P, T], U8, name="y_mxscale_%d" % g, align_bytes=64))
 
         def round_y(i):
-            n = units[i][2]
-            tile = work.tile([P, n * PACK], BF16, name="y_grouped", bufs=2, align_bytes=64)
-            y_grouped[i] = tile
-            if FOURCOL:
-                nc.vector.tensor_copy(
-                    out=tile[:].rearrange("p (c i t) -> p c t i", t=PACK, i=4),
-                    in_=y_tiles[i][:].rearrange("p t (c i) -> p c t i", i=4),
-                )
-            else:
-                nc.vector.tensor_copy(
-                    out=tile[:].rearrange("p (m t) -> p m t", t=PACK), in_=y_tiles[i][:].rearrange("p t m -> p m t")
-                )
+            y_grouped[i] = work.tile([P, units[i][2] * PACK], BF16, name="y_grouped", bufs=2, align_bytes=64)
+            nc.vector.tensor_copy(
+                out=y_grouped[i][:].rearrange("p (c a t) -> p c t a", t=PACK, a=4),
+                in_=y_tiles[i][:].rearrange("p t (c a) -> p c t a", a=4),
+            )
 
         def quantise_y(i):
-            g, tok, n = units[i]
-            toks = slice(tok, tok + n)
+            g, first, n = units[i]
+            steps = slice(first, first + n)
             codes = work.tile([P, n], U32, name="y_codes", bufs=3, align_bytes=64)
-            nc.vector.quantize_mx(out=codes[:].bitcast(FP8X4), scales=y_planes[g][:, toks], in_=y_grouped[i][:])
+            nc.vector.quantize_mx(out=codes[:].bitcast(FP8X4), scales=y_mxscale[g][:, steps], in_=y_grouped[i][:])
             words = out_1[g].rearrange("p m t -> p (m t)").bitcast(I32)
-            nc.sync.dma_start(out=words[:, toks], in_=codes[:].bitcast(I32))
-            if tok + n == T:
-                for q in range(4):
-                    queue = nc.scalar if (g == NGROUP - 1 and q % 2 == 1) else nc.sync
-                    queue.dma_start(
-                        out=out_2[g, 4 * q : 4 * q + 4, :].bitcast(I32),
-                        in_=y_planes[g][32 * q : 32 * q + 4, :].bitcast(I32),
-                    )
+            nc.sync.dma_start(out=words[:, steps], in_=codes[:].bitcast(I32))
 
-        widen(0, False)
-        widen(1, True)
-        widen(2, True)
-        turn_x(0)
-        empty_x(0)
+        def store_scales(g, steps, queues=(nc.sync, nc.sync)):
+            for q in range(4):
+                queues[q % 2].dma_start(
+                    out=out_2[g, 4 * q : 4 * q + 4, steps].bitcast(I32),
+                    in_=y_mxscale[g][32 * q : 32 * q + 4, steps].bitcast(I32),
+                )
+
+        widen(0)
+        widen(1)
+        widen(2, on_scalar=True)
+        for s in range(3):
+            turn_x(s)
+            empty_x(s)
         group_w(0, 0)
-        group_w(1, 0)
-        turn_x(1)
-        empty_x(1)
-        turn_x(2)
-        empty_x(2)
-        quantise_w(0, 0)
         quantise_x(0)
-        quantise_w(1, 0)
-        group_w(2, 0, True)
         quantise_x(1)
+        quantise_w(0, 0)
+        for k in range(PACK):
+            tap_pass(0, k, FILTER, 0, 0)
+        group_w(1, 0)
+        widen(3, on_scalar=True)
+        group_w(2, 0, on_scalar=True)
         quantise_x(2)
-        for t in range(PACK):
-            conv(0, t, 0)
+        quantise_w(1, 0)
+        for k in range(PACK):
+            tap_pass(0, k, FILTER, 0, 1)
+            activate(0, k, FILTER)
         group_w(3, 0)
         quantise_w(2, 0)
         quantise_w(3, 0)
-        widen(3, False)
-        widen(4, False)
-        conv(0, 0, 1)
-        conv(0, 1, 1)
-        turn_x(3)
-        turn_x(4)
-        empty_x(3)
-        empty_x(4)
-        widen(5, False)
+        widen(4)
+        for k in range(2):
+            tap_pass(0, k, GATE, 0, 0)
+        for k in range(2):
+            tap_pass(0, k, GATE, 0, 1)
+            activate(0, k, GATE)
+        for s in (3, 4):
+            turn_x(s)
+        for s in (3, 4):
+            empty_x(s)
+        widen(5)
         product(0, 0)
-        widen(6, False)
+        widen(6)
         quantise_x(3)
         quantise_x(4)
-        conv(0, 2, 1)
-        conv(0, 3, 1)
+        convolve(0, 2, (GATE,))
+        convolve(0, 3, (GATE,))
         product(0, 1)
-        turn_x(5)
-        turn_x(6)
-        empty_x(5)
-        empty_x(6)
+        for s in (5, 6):
+            turn_x(s)
+        for s in (5, 6):
+            empty_x(s)
         product(0, 2)
 
-        def item(kind, k):
-            if kind == "w":
-                return (lambda: group_w(k, 1), lambda: quantise_w(k, 1))
-            return (lambda: round_y(k), lambda: quantise_y(k))
+        def quantise_plane(i):
+            quantise_y(i)
+            if i == NCHUNK - 1:
+                store_scales(0, slice(0, T))
 
-        full = NGROUP * NCHUNK - 1
-        for i in range(1, full):
-            items = [item(kind, k) for kind, k in ITEMS[i - 1]]
-            side = [[], [], [], []]
-            if i in (1, 2):
-                side[0].extend([lambda: quantise_x(2 * i + 3), lambda: quantise_x(2 * i + 4)])
-            side[0].append(items[0][0])
-            side[1].append(items[0][1])
-            if len(items) > 1:
-                side[2].append(items[1][0])
-                side[3].append(items[1][1])
-            if i == 1:
-                side[2].extend([lambda: widen(7, False), lambda: widen(8, False)])
-            n_s = Y_EVAC_SCALAR[i - 1]
-            gate(i, 0)
-            gate(i, 1)
+        def weight_job(w):
+            return (lambda: group_w(w, 1), lambda: quantise_w(w, 1))
+
+        def plane_job(i):
+            return (lambda: round_y(i), lambda: quantise_plane(i))
+
+        jobs = [weight_job(w) for w in range(len(weights))] + [plane_job(i) for i in range(last_full)]
+        last_segments = (NSEG - 2, NSEG - 1)
+
+        for i in range(1, last_full + 1):
+            mine = [jobs.pop(0) for slot in range(min(len(jobs), 1 if i == 1 else 2))]
+            on_scalar = 4 - i % 2 if len(mine) == 2 else 2
+
+            convolve(i, 0)
+            convolve(i, 1)
             product(i - 1, 3)
-            if LATE:
-                gate(i, 2)
+            convolve(i, 2)
             turn_y(i - 1)
-            for f in side[0]:
-                f()
+            if i <= 2:
+                quantise_x(2 * i + 3)
+                quantise_x(2 * i + 4)
+            mine[0][0]()
             product(i, 0)
-            for f in side[1]:
-                f()
+            mine[0][1]()
             product(i, 1)
-            if LATE:
-                for f in side[2]:
-                    f()
-            for j in range(n_s):
-                empty_y(i - 1, j, True)
-            for j in range(n_s, 4):
-                empty_y(i - 1, j, False)
-            if not LATE:
-                gate(i, 2)
-            gate(i, 3)
-            if not LATE:
-                for f in side[2]:
-                    f()
+            if len(mine) == 2:
+                mine[1][0]()
             if i == 1:
-                turn_x(7)
-                turn_x(8)
-                empty_x(7)
-                empty_x(8)
+                for s in last_segments:
+                    widen(s)
+            store_rows(i - 1, on_scalar)
+            convolve(i, 3)
+            if i == 1:
+                for s in last_segments:
+                    turn_x(s)
+                for s in last_segments:
+                    empty_x(s)
             product(i, 2)
-            for f in side[3]:
-                f()
+            if len(mine) == 2:
+                mine[1][1]()
 
-        a, b = full, full + 1
-        gate(a, 0)
-        gate(a, 1)
-        product(a - 1, 3)
-        turn_y(a - 1)
-        round_y(a - 1)
+        a, b = last_full + 1, last_full + 2
+        convolve(a, 0)
+        convolve(a, 1)
+        product(last_full, 3)
+        turn_y(last_full)
         product(a, 0)
-        quantise_y(a - 1)
+        round_y(last_full)
         product(a, 1)
-        n_s = Y_EVAC_SCALAR[a - 1]
-        for j in range(4):
-            empty_y(a - 1, j, j < n_s)
-        gate(b, 0)
-        gate(b, 1)
+        for j in range(3):
+            store_row_bank(last_full, j, True)
+        quantise_y(last_full)
+        store_scales(1, slice(0, T - BANK))
+        store_row_bank(last_full, 3, False)
+        convolve(b, 0)
+        convolve(b, 1)
         turn_y(a)
         round_y(a)
         product(b, 0)
@@ -377,9 +364,8 @@ def tile_dilated_gated_activation_b1_kernel(
         turn_y(b, (0, 1))
         product(b, 1)
         turn_y(b, (2, 3))
-        empty_y(a, 0, True)
-        empty_y(a, 1, True)
+        store_rows(a, 2)
         round_y(b)
-        empty_y(b, 0, True)
-        empty_y(b, 1, True)
+        store_rows(b, 2)
         quantise_y(b)
+        store_scales(1, slice(T - BANK, T), (nc.sync, nc.scalar))

from contextlib import ExitStack

import concourse.mybir as mybir
from concourse.masks import make_identity

T, D, C, N = 2048, 256, 512, 1024
FLOPS = 4 * 2 * T * C * N

F32 = mybir.dt.float32
BF16 = mybir.dt.bfloat16
U32 = mybir.dt.uint32
I32 = mybir.dt.int32
U8 = mybir.dt.uint8
FP8 = mybir.dt.float8_e4m3fn
FP8X4 = mybir.dt.float8_e4m3fn_x4
ACT = mybir.ActivationFunctionType
ALU = mybir.AluOpType

P = 128
PACK = 4
GROUP = P * PACK
NGROUP = N // GROUP
BANK = 512
NCHUNK = T // BANK
SEG = 256
NSEG = (T + D) // SEG
SCALE_SPAN = 128
NSCALE = C // SCALE_SPAN
FILTER, GATE = 0, 1


def tile_dilated_gated_activation_b1_kernel(
    tc, X_bytes, X_scale, Wf_past, Wf_now, Wg_past, Wg_now, gain, out_0, out_1, out_2
):
    nc = tc.nc
    weights = (Wf_past, Wf_now, Wg_past, Wg_now)

    with ExitStack() as ctx:
        keep = ctx.enter_context(tc.tile_pool(name="keep", bufs=1))
        work = ctx.enter_context(tc.tile_pool(name="work", bufs=2))
        psum = ctx.enter_context(tc.psum_pool(name="psum", bufs=4))
        ctx.enter_context(tc.manual_schedule())

        ident = keep.tile([P, P], F32, name="ident")
        make_identity(nc, ident[:])
        warm_in = keep.tile([P, 1], F32, name="warm_in")
        warm_out = keep.tile([P, 1], F32, name="warm_out")
        nc.vector.memset(warm_in[:], 0.0)
        nc.scalar.activation(out=warm_out[:], in_=warm_in[:], func=ACT.Sigmoid)

        byte_rows = X_bytes.rearrange("(s p e) k -> p s (e k)", p=P, e=2)
        scale_rows = X_scale.rearrange("(s p e) b -> p s (e b)", p=P, e=2)
        x_bytes, x_scale, w_raw = {}, {}, {}

        def load_bytes(first, last):
            tile = keep.tile([P, last - first, 2 * C], U8, name="x_bytes_%d" % first)
            nc.sync.dma_start(out=tile[:], in_=byte_rows[:, first:last, :])
            for s in range(first, last):
                x_bytes[s] = tile[:, s - first, :]

        def load_scale(first, last):
            tile = keep.tile([P, last - first, 2 * NSCALE], F32, name="x_scale_%d" % first)
            nc.sync.dma_start(out=tile[:], in_=scale_rows[:, first:last, :])
            for s in range(first, last):
                x_scale[s] = tile[:, s - first, :]

        def load_weight(w, g):
            tile = keep.tile([P, PACK, GROUP], BF16, name="w_raw_%d_%d" % (w, g))
            columns = weights[w][:, g * GROUP : (g + 1) * GROUP]
            nc.sync.dma_start(out=tile[:], in_=columns.rearrange("(p j) n -> p j n", j=PACK))
            w_raw[w, g] = tile

        load_scale(0, 5)
        load_bytes(0, 3)
        load_weight(0, 0)
        load_weight(1, 0)
        load_bytes(3, 5)
        load_weight(2, 0)
        load_weight(3, 0)
        load_scale(5, NSEG)
        gains = keep.tile([P, NGROUP, PACK], BF16, name="gains")
        nc.sync.dma_start(out=gains[:], in_=gain.rearrange("o (g p t) -> p (o g) t", p=P, t=PACK))
        load_bytes(5, NSEG)
        for w in range(len(weights)):
            load_weight(w, 1)

        x_codes = keep.tile([P, T + D], U32, name="x_codes", align_bytes=64)
        x_mxscale = keep.tile([P, T + D], U8, name="x_mxscale", align_bytes=64)
        x_words, x_bank, x_grouped = {}, {}, {}

        def widen(s, on_scalar=False):
            tile = work.tile([P, 2, C], BF16, name="x_wide", bufs=4)
            x_words[s] = []
            for e in range(2):
                for b in range(NSCALE):
                    span = slice(SCALE_SPAN * b, SCALE_SPAN * (b + 1))
                    src = x_bytes[s][:, e * C : (e + 1) * C][:, span].bitcast(FP8)
                    scale = x_scale[s][:, NSCALE * e + b : NSCALE * e + b + 1]
                    if on_scalar:
                        nc.scalar.activation(out=tile[:, e, span], in_=src, func=ACT.Copy, scale=scale)
                    else:
                        dst = tile[:, e, :].rearrange("q (u p h) -> q p u h", u=2, h=2)
                        nc.vector.tensor_scalar(
                            out=dst[:, SCALE_SPAN // PACK * b : SCALE_SPAN // PACK * (b + 1), :, :],
                            in0=src.rearrange("q (p u h) -> q p u h", u=2, h=2),
                            scalar1=scale,
                            scalar2=None,
                            op0=ALU.mult,
                        )
                words = tile[:, e, :].bitcast(F32)
                if on_scalar:
                    x_words[s].append([words[:, u : 2 * P : 2] for u in range(2)])
                else:
                    x_words[s].append([words[:, u * P : (u + 1) * P] for u in range(2)])

        def turn_x(s):
            x_bank[s] = psum.tile([P, 2, 2, P], F32, name="turn_bank")
            for e in range(2):
                for u in range(2):
                    nc.tensor.transpose(x_bank[s][:, e, u, :], x_words[s][e][u], ident[:])

        def empty_x(s):
            x_grouped[s] = work.tile([P, SEG * PACK], BF16, name="x_grouped", bufs=4, align_bytes=64)
            nc.scalar.copy(
                out=x_grouped[s][:].bitcast(F32).rearrange("p (r e u) -> p r e u", e=2, u=2),
                in_=x_bank[s][:].rearrange("p e u r -> p r e u"),
            )

        def quantise_x(s):
            cols = slice(s * SEG, (s + 1) * SEG)
            nc.vector.quantize_mx(out=x_codes[:, cols].bitcast(FP8X4), scales=x_mxscale[:, cols], in_=x_grouped[s][:])

        w_grouped, w_codes, w_mxscale = {}, {}, {}

        def group_w(w, g, on_scalar=False):
            w_grouped[w, g] = work.tile([P, GROUP * PACK], BF16, name="w_grouped", bufs=3, align_bytes=64)
            dst = w_grouped[w, g][:].rearrange("p (t a b j) -> p a j b t", t=PACK, b=2, j=PACK)
            src = w_raw[w, g][:].rearrange("p j (a b t) -> p a j b t", b=2, t=PACK)
            if on_scalar:
                nc.scalar.copy(out=dst, in_=src)
            else:
                nc.vector.tensor_copy(out=dst, in_=src)

        def quantise_w(w, g):
            w_codes[w, g] = keep.tile([P, GROUP], U32, name="w_codes_%d_%d" % (w, g), align_bytes=64)
            w_mxscale[w, g] = keep.tile([P, GROUP], U8, name="w_mxscale_%d_%d" % (w, g), align_bytes=64)
            nc.vector.quantize_mx(
                out=w_codes[w, g][:].bitcast(FP8X4), scales=w_mxscale[w, g][:], in_=w_grouped[w, g][:]
            )

        units = [(g, c * BANK, BANK) for g in range(NGROUP) for c in range(NCHUNK)][:-1]
        last_full = len(units) - 1
        units.extend([(NGROUP - 1, T - BANK, BANK // 2), (NGROUP - 1, T - BANK // 2, BANK // 2)])
        conv_banks, acts, y_tiles, y_banks, y_grouped = {}, {}, {}, {}, {}

        def tap_pass(i, k, conv, r, tap):
            g, first, n = units[i]
            if (i, k, conv) not in conv_banks:
                conv_banks[i, k, conv] = psum.tile([P, BANK // n, n], F32, name="conv_bank")
            t = k * (BANK // n) + r
            cols = slice(t * P, (t + 1) * P)
            steps = slice(first + tap * D, first + n + tap * D)
            nc.tensor.matmul_mx(
                out=conv_banks[i, k, conv][:, r, :],
                lhsT=w_codes[2 * conv + tap, g][:, cols].bitcast(FP8X4),
                lhsT_scale=w_mxscale[2 * conv + tap, g][:, cols],
                rhs=x_codes[:, steps].bitcast(FP8X4),
                rhs_scale=x_mxscale[:, steps],
                start=(tap == 0),
                stop=(tap == 1),
            )

        def activate(i, k, conv):
            n = units[i][2]
            acts[i, k, conv] = work.tile([P, BANK // n, n], F32, name=("tanh_f", "sigmoid_h")[conv], bufs=4)
            nc.scalar.activation(
                out=acts[i, k, conv][:], in_=conv_banks[i, k, conv][:], func=(ACT.Tanh, ACT.Sigmoid)[conv]
            )

        def convolve(i, k, convs=(FILTER, GATE)):
            for conv in convs:
                for r in range(BANK // units[i][2]):
                    for tap in range(2):
                        tap_pass(i, k, conv, r, tap)
                activate(i, k, conv)

        def product(i, k):
            g, first, n = units[i]
            if k == 0:
                y_tiles[i] = work.tile([P, PACK, n], F32, name="y_tile", bufs=6)
            for r in range(BANK // n):
                t = k * (BANK // n) + r
                nc.vector.scalar_tensor_tensor(
                    out=y_tiles[i][:, t, :],
                    in0=acts[i, k, FILTER][:, r, :],
                    scalar=gains[:, g, t : t + 1],
                    in1=acts[i, k, GATE][:, r, :],
                    op0=ALU.mult,
                    op1=ALU.mult,
                )

        def turn_y(i, slots=range(PACK)):
            for j in range(units[i][2] // P):
                if (i, j) not in y_banks:
                    y_banks[i, j] = psum.tile([P, PACK, P], F32, name="turn_bank")
                for t in slots:
                    nc.tensor.transpose(y_banks[i, j][:, t, :], y_tiles[i][:, t, j * P : (j + 1) * P], ident[:])

        def store_rows(i, on_scalar):
            g, first, n = units[i]
            for j in range(n // P):
                store_row_bank(i, j, j < on_scalar)

        def store_row_bank(i, j, on_scalar):
            g, first, n = units[i]
            tile = work.tile([P, GROUP], F32, name="y_rows", bufs=8)
            dst = tile[:].rearrange("q (p t) -> q p t", t=PACK)
            src = y_banks[i, j][:].rearrange("q t p -> q p t")
            if on_scalar:
                nc.scalar.copy(out=dst, in_=src)
            else:
                nc.vector.tensor_copy(out=dst, in_=src)
            row = first + j * P
            nc.sync.dma_start(out=out_0[row : row + P, g * GROUP : (g + 1) * GROUP], in_=tile[:])

        y_mxscale = []
        for g in range(NGROUP):
            y_mxscale.append(keep.tile([P, T], U8, name="y_mxscale_%d" % g, align_bytes=64))

        def round_y(i):
            y_grouped[i] = work.tile([P, units[i][2] * PACK], BF16, name="y_grouped", bufs=2, align_bytes=64)
            nc.vector.tensor_copy(
                out=y_grouped[i][:].rearrange("p (c a t) -> p c t a", t=PACK, a=4),
                in_=y_tiles[i][:].rearrange("p t (c a) -> p c t a", a=4),
            )

        def quantise_y(i):
            g, first, n = units[i]
            steps = slice(first, first + n)
            codes = work.tile([P, n], U32, name="y_codes", bufs=3, align_bytes=64)
            nc.vector.quantize_mx(out=codes[:].bitcast(FP8X4), scales=y_mxscale[g][:, steps], in_=y_grouped[i][:])
            words = out_1[g].rearrange("p m t -> p (m t)").bitcast(I32)
            nc.sync.dma_start(out=words[:, steps], in_=codes[:].bitcast(I32))

        def store_scales(g, steps, queues=(nc.sync, nc.sync)):
            for q in range(4):
                queues[q % 2].dma_start(
                    out=out_2[g, 4 * q : 4 * q + 4, steps].bitcast(I32),
                    in_=y_mxscale[g][32 * q : 32 * q + 4, steps].bitcast(I32),
                )

        widen(0)
        widen(1)
        widen(2, on_scalar=True)
        for s in range(3):
            turn_x(s)
            empty_x(s)
        group_w(0, 0)
        quantise_x(0)
        quantise_x(1)
        quantise_w(0, 0)
        for k in range(PACK):
            tap_pass(0, k, FILTER, 0, 0)
        group_w(1, 0)
        widen(3, on_scalar=True)
        group_w(2, 0, on_scalar=True)
        quantise_x(2)
        quantise_w(1, 0)
        for k in range(PACK):
            tap_pass(0, k, FILTER, 0, 1)
            activate(0, k, FILTER)
        group_w(3, 0)
        quantise_w(2, 0)
        quantise_w(3, 0)
        widen(4)
        for k in range(2):
            tap_pass(0, k, GATE, 0, 0)
        for k in range(2):
            tap_pass(0, k, GATE, 0, 1)
            activate(0, k, GATE)
        for s in (3, 4):
            turn_x(s)
        for s in (3, 4):
            empty_x(s)
        widen(5)
        product(0, 0)
        widen(6)
        quantise_x(3)
        quantise_x(4)
        convolve(0, 2, (GATE,))
        convolve(0, 3, (GATE,))
        product(0, 1)
        for s in (5, 6):
            turn_x(s)
        for s in (5, 6):
            empty_x(s)
        product(0, 2)

        def quantise_plane(i):
            quantise_y(i)
            if i == NCHUNK - 1:
                store_scales(0, slice(0, T))

        def weight_job(w):
            return (lambda: group_w(w, 1), lambda: quantise_w(w, 1))

        def plane_job(i):
            return (lambda: round_y(i), lambda: quantise_plane(i))

        jobs = [weight_job(w) for w in range(len(weights))] + [plane_job(i) for i in range(last_full)]
        last_segments = (NSEG - 2, NSEG - 1)

        for i in range(1, last_full + 1):
            mine = [jobs.pop(0) for slot in range(min(len(jobs), 1 if i == 1 else 2))]
            on_scalar = 4 - i % 2 if len(mine) == 2 else 2

            convolve(i, 0)
            convolve(i, 1)
            product(i - 1, 3)
            convolve(i, 2)
            turn_y(i - 1)
            if i <= 2:
                quantise_x(2 * i + 3)
                quantise_x(2 * i + 4)
            mine[0][0]()
            product(i, 0)
            mine[0][1]()
            product(i, 1)
            if len(mine) == 2:
                mine[1][0]()
            if i == 1:
                for s in last_segments:
                    widen(s)
            store_rows(i - 1, on_scalar)
            convolve(i, 3)
            if i == 1:
                for s in last_segments:
                    turn_x(s)
                for s in last_segments:
                    empty_x(s)
            product(i, 2)
            if len(mine) == 2:
                mine[1][1]()

        a, b = last_full + 1, last_full + 2
        convolve(a, 0)
        convolve(a, 1)
        product(last_full, 3)
        turn_y(last_full)
        product(a, 0)
        round_y(last_full)
        product(a, 1)
        for j in range(3):
            store_row_bank(last_full, j, True)
        quantise_y(last_full)
        store_scales(1, slice(0, T - BANK))
        store_row_bank(last_full, 3, False)
        convolve(b, 0)
        convolve(b, 1)
        turn_y(a)
        round_y(a)
        product(b, 0)
        quantise_y(a)
        turn_y(b, (0, 1))
        product(b, 1)
        turn_y(b, (2, 3))
        store_rows(a, 2)
        round_y(b)
        store_rows(b, 2)
        quantise_y(b)
        store_scales(1, slice(T - BANK, T), (nc.sync, nc.scalar))
